import numpy as np
import ml_dtypes


def mxq(x, axis, fmt="e4m3"):
    dtype, down = {"e4m3": (ml_dtypes.float8_e4m3fn, 7), "e5m2": (ml_dtypes.float8_e5m2, 14)}[fmt]
    v = np.moveaxis(np.asarray(x, np.float32).astype(ml_dtypes.bfloat16).astype(np.float64), axis, -1)
    blocks = v.reshape(v.shape[:-1] + (-1, 32))
    amax = np.abs(blocks).max(-1, keepdims=True)
    byte = np.maximum(np.where(amax > 0, np.frexp(amax)[1] - 1 + 127, 0) - down, 1)
    scale = np.exp2(byte - 127.0)
    codes = (blocks / scale).astype(np.float32).astype(dtype).astype(np.float64)
    return np.moveaxis((codes * scale).reshape(v.shape), -1, axis)


WIDE = False


def mx_kscale(k):
    if not WIDE:
        return np.ones(k)
    levels = np.array([30, -30])
    if k % 512:
        return np.exp2(np.random.permutation(np.resize(levels, k // 32))).repeat(32)
    a = np.empty((k // 512, 16))
    for p in range(k // 512):
        a[p, :8] = np.random.permutation(np.resize(levels, 8))
        for g in range(8):
            far = levels[np.abs(levels - a[p, g]) >= 10]
            a[p, g + 8] = far[np.random.randint(len(far))]
    return np.exp2(a.ravel()).repeat(32)


def f64(x):
    return np.asarray(x).astype(np.float64)


def striped(idx):
    return np.tile(np.asarray(idx).reshape(-1, 16).T, (8, 1)).astype(np.uint16)


def unstriped(offs):
    return offs[:16].T.reshape(-1).astype(np.int64)


def striped8(idx):
    return np.asarray(idx).reshape(8, -1, 16).transpose(0, 2, 1).reshape(128, -1).astype(np.uint16)


def unstriped8(offs):
    return offs.reshape(8, 16, -1).transpose(0, 2, 1).reshape(8, -1).astype(np.int64)


def pick8(x, idx, run):
    r = np.arange(len(x))
    return x[r[:, None], idx[r % (8 * run) // run]]


E2M1 = np.array([0.0, 0.5, 1.0, 1.5, 2.0, 3.0, 4.0, 6.0, -0.0, -0.5, -1.0, -1.5, -2.0, -3.0, -4.0, -6.0])


def pack_weight(w, fmt):
    k, n = w.shape
    w = f64(np.asarray(w, np.float32).astype(ml_dtypes.bfloat16)).reshape(k // 32, 32, n)
    amax = np.abs(w).max(1)
    if fmt in ("e4m3", "e5m2"):
        byte = np.frexp(amax)[1] - 1 + 127 - (7 if fmt == "e4m3" else 14)
    else:
        mant, ex = np.frexp(amax / 6.0)
        byte = np.where(mant > 0.5, ex, ex - 1) + 127
    byte = np.clip(np.where(amax > 0, byte, 1), 1, 254)
    scaled = (w * np.exp2(127.0 - byte)[:, None, :]).reshape(k, n).astype(np.float32)
    by_word = np.ascontiguousarray(scaled.reshape(k // 512, 128, 4, n).transpose(0, 1, 3, 2))
    if fmt in ("e4m3", "e5m2"):
        words = by_word.astype(ml_dtypes.float8_e4m3fn if fmt == "e4m3" else ml_dtypes.float8_e5m2).view(np.uint8)
    else:
        c = by_word.astype(ml_dtypes.float4_e2m1fn).view(np.uint8) & 0xF
        words = (c[..., 0::2] | (c[..., 1::2] << 4)).reshape(k // 512, 128, 2 * n)
    return np.ascontiguousarray(words), np.ascontiguousarray(byte.astype(np.uint8).reshape(k // 512, 16, n))


def unpack_weight(words, scales, fmt):
    g, _, n = scales.shape
    words = np.ascontiguousarray(words).reshape(g, 128, n, -1)
    if fmt in ("e4m3", "e5m2"):
        vals = words.view(ml_dtypes.float8_e4m3fn if fmt == "e4m3" else ml_dtypes.float8_e5m2).astype(np.float64)
    else:
        nib = np.empty((g, 128, n, 4), np.uint8)
        nib[..., 0::2] = words & 0xF
        nib[..., 1::2] = words >> 4
        vals = E2M1[nib]
    vals = vals * np.repeat(np.exp2(scales.astype(np.float64) - 127.0), 8, axis=1)[..., None]
    return vals.transpose(0, 1, 3, 2).reshape(g * 512, n)


K, T, J, R, C, D, O, N, E = 512, 1024, 256, 512, 512, 512, 256, 256, 512


def setup_inputs():
    n = np.random.standard_normal
    idx = np.random.permutation(T)[:J]
    idx2 = np.stack([np.random.permutation(C)[:J] for _ in range(8)])
    idx3 = np.stack([np.random.permutation(D)[:J] for _ in range(8)])
    idx4 = np.random.permutation(C)[:O]
    idx5 = np.random.permutation(D)[:O]
    idx6 = np.stack([np.random.permutation(E)[:O] for _ in range(8)])
    idx7 = np.random.permutation(E)[:O]
    fk = mx_kscale(K)
    fr = mx_kscale(R)
    xtp = pack_weight(n((K, T)) / fk[:, None], "e5m2")
    wp = pack_weight(n((K, R)) * 1 / np.sqrt(K) * fk[:, None] * fr, "e2m1")
    w2p = pack_weight(n((K, R)) * 1 / np.sqrt(K) * fk[:, None] * fr, "e4m3")
    wbp = pack_weight(n((R, N)) * 1 / np.sqrt(R) / fr[:, None], "e2m1")
    return {
        "xt_words": xtp[0],
        "xt_scales": xtp[1],
        "w_words": wp[0],
        "w_scales": wp[1],
        "w2_words": w2p[0],
        "w2_scales": w2p[1],
        "sa": (np.random.uniform(0.5, 1.6, (R, 1))).astype(np.float32),
        "sb": (np.random.uniform(0.5, 1.6, (R, 1))).astype(np.float32),
        "wb_words": wbp[0],
        "wb_scales": wbp[1],
        "offs": striped(idx),
        "offs2": striped8(idx2),
        "offs3": striped8(idx3),
        "offs4": striped(idx4),
        "offs5": striped(idx5),
        "offs6": striped8(idx6),
        "offs7": striped(idx7),
    }


def reference(xt_words, xt_scales, w_words, w_scales, w2_words, w2_scales, sa, sb, wb_words, wb_scales, offs, offs2, offs3, offs4, offs5, offs6, offs7):
    idx = unstriped(offs)
    idx2 = unstriped8(offs2)
    idx3 = unstriped8(offs3)
    idx4 = unstriped(offs4)
    idx5 = unstriped(offs5)
    idx6 = unstriped8(offs6)
    idx7 = unstriped(offs7)
    xtu = unpack_weight(xt_words, xt_scales, "e5m2")
    wu = unpack_weight(w_words, w_scales, "e2m1")
    w2u = unpack_weight(w2_words, w2_scales, "e4m3")
    wbu = unpack_weight(wb_words, wb_scales, "e2m1")
    xtidxg = xtu[:, idx]
    a = wu.T @ xtidxg
    b = w2u.T @ xtidxg
    pw = np.zeros((R, C))
    pw[np.arange(R)[:, None], idx2[np.arange(R) % 512 // 64]] = a
    pv = np.zeros((R, D))
    pv[np.arange(R)[:, None], idx3[np.arange(R) % 512 // 64]] = b
    hid = np.abs(pw[:, idx4] * f64(sa) - pv[:, idx5] * f64(sb))
    hidq = mxq(hid, 0, "e4m3")
    p = wbu.T @ hidq
    pa = np.zeros((N, E))
    pa[np.arange(N)[:, None], idx6[np.arange(N) % 128 // 16]] = p
    pb = np.zeros((N, E))
    pb[:, idx7] = p
    y = pa + pb
    return y

@@ -1,0 +1,211 @@
+from contextlib import ExitStack
+
+import concourse.mybir as mybir
+
+K, T, J, R, C, O, N, E = 512, 1024, 256, 512, 512, 256, 256, 512
+FLOPS = 2 * K * R * J * 2 + 2 * R * N * O
+
+F32 = mybir.dt.float32
+BF16 = mybir.dt.bfloat16
+I32 = mybir.dt.int32
+U32 = mybir.dt.uint32
+U16 = mybir.dt.uint16
+U8 = mybir.dt.uint8
+E4M3X4 = mybir.dt.float8_e4m3fn_x4
+E5M2X4 = mybir.dt.float8_e5m2_x4
+E2M1X4 = mybir.dt.float4_e2m1fn_x4
+COPY = mybir.ActivationFunctionType.Copy
+ALU = mybir.AluOpType
+
+P = 128
+PACK = 4
+HALF = 128
+HALF_COLS = HALF // 16
+
+
+def tile_list_twoownboards_twow_one_owntwopages_kernel(
+    tc, xt_words, xt_scales, w_words, w_scales, w2_words, w2_scales, sa, sb, wb_words, wb_scales,
+    offs, offs2, offs3, offs4, offs5, offs6, offs7, out,
+):
+    nc = tc.nc
+    with ExitStack() as ctx:
+        lists = ctx.enter_context(tc.tile_pool(name="lists", bufs=1))
+        keep = ctx.enter_context(tc.tile_pool(name="keep", bufs=1))
+        first = ctx.enter_context(tc.psum_pool(name="first", bufs=4))
+        second = ctx.enter_context(tc.psum_pool(name="second", bufs=1))
+
+        def load_list(src, name):
+            t = lists.tile([P, 16], U16, name=name)
+            nc.sync.dma_start(t[:], src)
+            return t
+
+        def half(lst, h):
+            return lst[:, h * HALF_COLS : (h + 1) * HALF_COLS]
+
+        def load_scale_rows(plane, src):
+            for q in range(4):
+                nc.sync.dma_start(plane[32 * q : 32 * q + 4, :].bitcast(I32), src[0, 4 * q : 4 * q + 4, :].bitcast(I32))
+
+        xt_plane = keep.tile([P, T], U8, name="xt_plane", tag="xt_plane", align_bytes=64)
+        nc.vector.memset(xt_plane[:].bitcast(I32), 0)
+        w_plane = keep.tile([P, R], U8, name="w_plane", tag="w_plane", align_bytes=64)
+        nc.vector.memset(w_plane[:].bitcast(I32), 0)
+
+        xt_tab = keep.tile([P, T], U32, name="xt_tab", tag="xt_tab", align_bytes=64)
+        nc.scalar.dma_start(xt_tab[:].bitcast(I32), xt_words[0].rearrange("p n t -> p (n t)").bitcast(I32))
+        w_raw = keep.tile([P, 2 * R], U8, name="w_raw", tag="w_raw", align_bytes=64)
+        nc.scalar.dma_start(w_raw[:].bitcast(I32), w_words[0].bitcast(I32))
+
+        xt_stage = keep.tile([4, 4, T // 4], I32, name="xt_stage", align_bytes=64)
+        nc.sync.dma_start(xt_stage[:], xt_scales[0].bitcast(I32).rearrange("(q r) c -> r q c", q=4))
+        w_stage = keep.tile([4, 4, R // 4], I32, name="w_stage", align_bytes=64)
+        nc.sync.dma_start(w_stage[:], w_scales[0].bitcast(I32).rearrange("(q r) c -> r q c", q=4))
+        l1 = load_list(offs, "l1")
+        l2 = load_list(offs2, "l2")
+
+        for q in range(4):
+            nc.vector.tensor_copy(xt_plane[32 * q : 32 * q + 4, :].bitcast(I32), xt_stage[:, q, :])
+        for q in range(4):
+            nc.vector.tensor_copy(w_plane[32 * q : 32 * q + 4, :].bitcast(I32), w_stage[:, q, :])
+
+        w_codes = keep.tile([P, 2 * R], U8, name="w_codes", tag="w_codes", align_bytes=64)
+        w_sc = keep.tile([P, R], U8, name="w_sc", tag="w_sc", align_bytes=64)
+        w_raw_tm = w_raw[:].bitcast(U16).rearrange("p (m t) -> p t m", t=PACK)
+        w_codes_tm = w_codes[:].bitcast(U16).rearrange("p (t m) -> p t m", t=PACK)
+        w_plane_tm = w_plane[:].rearrange("p (m t) -> p t m", t=PACK)
+        w_sc_tm = w_sc[:].rearrange("p (t m) -> p t m", t=PACK)
+        nc.scalar.copy(w_codes_tm[:, 0, :], w_raw_tm[:, 0, :])
+        nc.vector.tensor_copy(w_sc_tm[:, 0, :], w_plane_tm[:, 0, :])
+
+        xg = keep.tile([P, J], U32, name="xg", align_bytes=64)
+        xg_sc = keep.tile([P, J], U8, name="xg_sc", align_bytes=64)
+
+        def page(name, tag):
+            t = keep.tile([P, C], F32, name=name, tag=tag, align_bytes=64)
+            nc.vector.memset(t[:], 0.0)
+            return t
+
+        def product(codes, scales, cols, dst):
+            width = cols.stop - cols.start
+            acc = first.tile([P, width], F32, name="acc")
+            nc.tensor.matmul_mx(
+                out=acc[:], lhsT=codes, lhsT_scale=scales,
+                rhs=xg[:, cols].bitcast(E5M2X4), rhs_scale=xg_sc[:, cols], start=True, stop=True,
+            )
+            nc.vector.tensor_copy(dst, acc[:])
+
+        def w_slice(t):
+            return w_codes[:, 2 * P * t : 2 * P * (t + 1)].bitcast(E2M1X4), w_sc[:, P * t : P * (t + 1)]
+
+        a_sb = [keep.tile([P, J], F32, name="a_sb%d" % t) for t in range(PACK)]
+        pw = [page("pw0", "pw0")]
+        for h in range(2):
+            cols = slice(h * HALF, (h + 1) * HALF)
+            nc.vector.tensor_copy(xg_sc[:, cols], xt_plane[:].indirect(half(l1, h)))
+            nc.vector.tensor_copy(xg[:, cols], xt_tab[:].indirect(half(l1, h)))
+            product(*w_slice(0), cols, a_sb[0][:, cols])
+            nc.scalar.activation(pw[0][:].indirect(half(l2, h)), a_sb[0][:, cols], COPY)
+            if h == 0:
+                nc.scalar.copy(w_codes_tm[:, 1:, :], w_raw_tm[:, 1:, :])
+        nc.vector.tensor_copy(w_sc_tm[:, 1:, :], w_plane_tm[:, 1:, :])
+        for t in range(1, PACK):
+            product(*w_slice(t), slice(0, J), a_sb[t][:])
+            pw.append(page("pw%d" % t, "pw%d" % t))
+            nc.scalar.activation(pw[t][:].indirect(l2[:]), a_sb[t][:], COPY)
+
+        w2_raw = keep.tile([P, R], I32, name="w2_raw", tag="w2_raw", align_bytes=64)
+        nc.sync.dma_start(w2_raw[:], w2_words[0].rearrange("p n t -> p (n t)").bitcast(I32))
+        w2_plane = keep.tile([P, R], U8, name="w2_plane", tag="w2_plane", align_bytes=64)
+        nc.vector.memset(w2_plane[:].bitcast(I32), 0)
+        load_scale_rows(w2_plane, w2_scales)
+        l3 = load_list(offs3, "l3")
+        sa_sb = keep.tile([P, PACK], F32, name="sa_sb")
+        nc.sync.dma_start(sa_sb[:], sa.rearrange("(p t) o -> p (t o)", t=PACK))
+        sb_sb = keep.tile([P, PACK], F32, name="sb_sb")
+        nc.sync.dma_start(sb_sb[:], sb.rearrange("(p t) o -> p (t o)", t=PACK))
+        l4 = load_list(offs4, "l4")
+        l5 = load_list(offs5, "l5")
+        wb_codes = keep.tile([P, 2 * N], U8, name="wb_codes", align_bytes=64)
+        nc.sync.dma_start(wb_codes[:].bitcast(I32), wb_words[0].bitcast(I32))
+        wb_sc = keep.tile([P, N], U8, name="wb_sc", align_bytes=64)
+        nc.vector.memset(wb_sc[:].bitcast(I32), 0)
+        load_scale_rows(wb_sc, wb_scales)
+        l6 = load_list(offs6, "l6")
+        l7 = load_list(offs7, "l7")
+
+        w2_codes = keep.tile([P, R], I32, name="w2_codes", align_bytes=64)
+        w2_sc = keep.tile([P, R], U8, name="w2_sc", align_bytes=64)
+        nc.vector.tensor_copy(
+            w2_codes[:].rearrange("p (t m) -> p m t", t=PACK), w2_raw[:].rearrange("p (m t) -> p m t", t=PACK)
+        )
+        nc.vector.tensor_copy(
+            w2_sc[:].rearrange("p (t m) -> p m t", t=PACK), w2_plane[:].rearrange("p (m t) -> p m t", t=PACK)
+        )
+
+        b_sb = [keep.tile([P, J], F32, name="b_sb%d" % t, tag="b_sb%d" % t) for t in range(PACK)]
+        pv = []
+        for t in range(PACK):
+            product(w2_codes[:, P * t : P * (t + 1)].bitcast(E4M3X4), w2_sc[:, P * t : P * (t + 1)], slice(0, J), b_sb[t][:])
+            pv.append(page("pv%d" % t, ("xt_tab", "xt_plane", "w_raw", "w_plane")[t]))
+
+        def fetch(picked, t, h):
+            nc.scalar.activation(picked[:, 0, t, :], pw[t][:].indirect(half(l4, h)), COPY, scale=sa_sb[:, t : t + 1])
+            nc.scalar.activation(picked[:, 1, t, :], pv[t][:].indirect(half(l5, h)), COPY, scale=sb_sb[:, t : t + 1])
+
+        def subtract(diff, picked, ts):
+            nc.vector.tensor_tensor(diff[:, ts, :], picked[:, 0, ts, :], picked[:, 1, ts, :], ALU.subtract)
+
+        def magnitude(hid, diff, ts):
+            d = diff[:, ts, :].rearrange("p t o -> p o t")
+            nc.vector.scalar_tensor_tensor(hid[:, :, ts], d, -1.0, d, ALU.mult, ALU.max)
+
+        def quantise(picked, h):
+            diff = keep.tile([P, PACK, HALF], F32, name="diff%d" % h)
+            hid = keep.tile([P, HALF, PACK], BF16, name="hid%d" % h, align_bytes=64)
+            subtract(diff, picked, slice(0, 2))
+            magnitude(hid, diff, slice(0, 2))
+            subtract(diff, picked, slice(2, 3))
+            subtract(diff, picked, slice(3, 4))
+            magnitude(hid, diff, slice(2, 4))
+            codes = keep.tile([P, HALF], U32, name="hid_codes%d" % h, align_bytes=64)
+            scales = keep.tile([P, HALF], U8, name="hid_sc%d" % h, align_bytes=64)
+            nc.vector.quantize_mx(out=codes[:].bitcast(E4M3X4), scales=scales[:], in_=hid[:].rearrange("p o t -> p (o t)"))
+            return codes, scales
+
+        def output_product(codes, scales, h):
+            acc = second.tile([P, 2, HALF], F32, name="acc2_%d" % h)
+            for m in range(2):
+                nc.tensor.matmul_mx(
+                    out=acc[:, m, :], lhsT=wb_codes[:, 2 * P * m : 2 * P * (m + 1)].bitcast(E2M1X4),
+                    lhsT_scale=wb_sc[:, P * m : P * (m + 1)],
+                    rhs=codes[:].bitcast(E4M3X4), rhs_scale=scales[:], start=True, stop=True,
+                )
+            p_sb = keep.tile([P, 2, HALF], F32, name="p_sb%d" % h)
+            nc.vector.tensor_copy(p_sb[:], acc[:])
+            return p_sb
+
+        picked0 = keep.tile([P, 2, PACK, HALF], F32, name="picked0")
+        for t in range(PACK):
+            nc.scalar.activation(pv[t][:].indirect(l3[:]), b_sb[t][:], COPY)
+            fetch(picked0, t, 0)
+        pa = [page("pa%d" % m, ("w2_raw", "w2_plane")[m]) for m in range(2)]
+        pb = [page("pb%d" % m, ("w_codes", "w_sc")[m]) for m in range(2)]
+        p0 = output_product(*quantise(picked0, 0), 0)
+
+        picked1 = keep.tile([P, 2, PACK, HALF], F32, name="picked1", tag="b_sb3")
+        for t in range(PACK):
+            fetch(picked1, t, 1)
+        hid1 = quantise(picked1, 1)
+        nc.vector.tensor_copy(pb[0][:].indirect(half(l7, 0)), p0[:, 0, :])
+        p1 = output_product(*hid1, 1)
+
+        for m in range(2):
+            nc.scalar.activation(pa[m][:].indirect(half(l6, 0)), p0[:, m, :], COPY)
+        nc.scalar.activation(pb[1][:].indirect(half(l7, 0)), p0[:, 1, :], COPY)
+        for m in range(2):
+            nc.scalar.activation(pa[m][:].indirect(half(l6, 1)), p1[:, m, :], COPY)
+            nc.vector.tensor_copy(pb[m][:].indirect(half(l7, 1)), p1[:, m, :])
+        for m in range(2):
+            res = keep.tile([P, E], F32, name="res%d" % m)
+            nc.vector.tensor_tensor(res[:], pa[m][:], pb[m][:], ALU.add)
+            nc.sync.dma_start(out[P * m : P * (m + 1), :], res[:])

@@ -47,35 +47,35 @@ def tile_list_twoownboards_twow_one_owntwopages_kernel(
                 nc.sync.dma_start(plane[32 * q : 32 * q + 4, :].bitcast(I32), src[0, 4 * q : 4 * q + 4, :].bitcast(I32))
 
         xt_plane = keep.tile([P, T], U8, name="xt_plane", tag="xt_plane", align_bytes=64)
-        nc.vector.memset(xt_plane[:].bitcast(I32), 0)
         w_plane = keep.tile([P, R], U8, name="w_plane", tag="w_plane", align_bytes=64)
         nc.vector.memset(w_plane[:].bitcast(I32), 0)
 
+        w2_plane = keep.tile([P, R], U8, name="w2_plane", tag="w2_plane", align_bytes=64)
+        nc.vector.memset(w2_plane[:].bitcast(I32), 0)
         xt_tab = keep.tile([P, T], U32, name="xt_tab", tag="xt_tab", align_bytes=64)
-        nc.scalar.dma_start(xt_tab[:].bitcast(I32), xt_words[0].rearrange("p n t -> p (n t)").bitcast(I32))
         w_raw = keep.tile([P, 2 * R], U8, name="w_raw", tag="w_raw", align_bytes=64)
-        nc.scalar.dma_start(w_raw[:].bitcast(I32), w_words[0].bitcast(I32))
 
-        xt_stage = keep.tile([4, 4, T // 4], I32, name="xt_stage", align_bytes=64)
-        nc.sync.dma_start(xt_stage[:], xt_scales[0].bitcast(I32).rearrange("(q r) c -> r q c", q=4))
         w_stage = keep.tile([4, 4, R // 4], I32, name="w_stage", align_bytes=64)
         nc.sync.dma_start(w_stage[:], w_scales[0].bitcast(I32).rearrange("(q r) c -> r q c", q=4))
         l1 = load_list(offs, "l1")
+        nc.scalar.dma_start(xt_tab[:].bitcast(I32), xt_words[0].rearrange("p n t -> p (n t)").bitcast(I32))
+        nc.scalar.dma_start(w_raw[:].bitcast(I32), w_words[0].bitcast(I32))
+        for q in range(4):
+            rows = xt_scales[0, 4 * q : 4 * q + 4, :].bitcast(I32)
+            nc.sync.dma_start(xt_plane[32 * q : 32 * q + 32, :].bitcast(I32), rows.unsqueeze(0).to_broadcast([8, 4, T // 4]))
         l2 = load_list(offs2, "l2")
 
         for q in range(4):
-            nc.vector.tensor_copy(xt_plane[32 * q : 32 * q + 4, :].bitcast(I32), xt_stage[:, q, :])
-        for q in range(4):
             nc.vector.tensor_copy(w_plane[32 * q : 32 * q + 4, :].bitcast(I32), w_stage[:, q, :])
 
-        w_codes = keep.tile([P, 2 * R], U8, name="w_codes", tag="w_codes", align_bytes=64)
-        w_sc = keep.tile([P, R], U8, name="w_sc", tag="w_sc", align_bytes=64)
+        w_codes0 = keep.tile([P, 2 * P], U8, name="w_codes0", align_bytes=64)
+        w_sc0 = keep.tile([P, P], U8, name="w_sc0", tag="w_sc0", align_bytes=64)
+        w_codes = keep.tile([P, 2 * (R - P)], U8, name="w_codes", tag="w_codes", align_bytes=64)
         w_raw_tm = w_raw[:].bitcast(U16).rearrange("p (m t) -> p t m", t=PACK)
-        w_codes_tm = w_codes[:].bitcast(U16).rearrange("p (t m) -> p t m", t=PACK)
+        w_codes_tm = w_codes[:].bitcast(U16).rearrange("p (t m) -> p t m", t=PACK - 1)
         w_plane_tm = w_plane[:].rearrange("p (m t) -> p t m", t=PACK)
-        w_sc_tm = w_sc[:].rearrange("p (t m) -> p t m", t=PACK)
-        nc.scalar.copy(w_codes_tm[:, 0, :], w_raw_tm[:, 0, :])
-        nc.vector.tensor_copy(w_sc_tm[:, 0, :], w_plane_tm[:, 0, :])
+        nc.scalar.copy(w_codes0[:].bitcast(U16), w_raw_tm[:, 0, :])
+        nc.vector.tensor_copy(w_sc0[:], w_plane_tm[:, 0, :])
 
         xg = keep.tile([P, J], U32, name="xg", align_bytes=64)
         xg_sc = keep.tile([P, J], U8, name="xg_sc", align_bytes=64)
@@ -95,7 +95,7 @@ def tile_list_twoownboards_twow_one_owntwopages_kernel(
             nc.vector.tensor_copy(dst, acc[:])
 
         def w_slice(t):
-            return w_codes[:, 2 * P * t : 2 * P * (t + 1)].bitcast(E2M1X4), w_sc[:, P * t : P * (t + 1)]
+            return w_codes[:, 2 * P * (t - 1) : 2 * P * t].bitcast(E2M1X4), w_sc[:, P * (t - 1) : P * t]
 
         a_sb = [keep.tile([P, J], F32, name="a_sb%d" % t) for t in range(PACK)]
         pw = [page("pw0", "pw0")]
@@ -103,11 +103,12 @@ def tile_list_twoownboards_twow_one_owntwopages_kernel(
             cols = slice(h * HALF, (h + 1) * HALF)
             nc.vector.tensor_copy(xg_sc[:, cols], xt_plane[:].indirect(half(l1, h)))
             nc.vector.tensor_copy(xg[:, cols], xt_tab[:].indirect(half(l1, h)))
-            product(*w_slice(0), cols, a_sb[0][:, cols])
+            product(w_codes0[:].bitcast(E2M1X4), w_sc0[:], cols, a_sb[0][:, cols])
             nc.scalar.activation(pw[0][:].indirect(half(l2, h)), a_sb[0][:, cols], COPY)
             if h == 0:
-                nc.scalar.copy(w_codes_tm[:, 1:, :], w_raw_tm[:, 1:, :])
-        nc.vector.tensor_copy(w_sc_tm[:, 1:, :], w_plane_tm[:, 1:, :])
+                nc.scalar.copy(w_codes_tm, w_raw_tm[:, 1:, :])
+        w_sc = keep.tile([P, R - P], U8, name="w_sc", tag="xt_plane", align_bytes=64)
+        nc.vector.tensor_copy(w_sc[:].rearrange("p (t m) -> p t m", t=PACK - 1), w_plane_tm[:, 1:, :])
         for t in range(1, PACK):
             product(*w_slice(t), slice(0, J), a_sb[t][:])
             pw.append(page("pw%d" % t, "pw%d" % t))
@@ -115,8 +116,6 @@ def tile_list_twoownboards_twow_one_owntwopages_kernel(
 
         w2_raw = keep.tile([P, R], I32, name="w2_raw", tag="w2_raw", align_bytes=64)
         nc.sync.dma_start(w2_raw[:], w2_words[0].rearrange("p n t -> p (n t)").bitcast(I32))
-        w2_plane = keep.tile([P, R], U8, name="w2_plane", tag="w2_plane", align_bytes=64)
-        nc.vector.memset(w2_plane[:].bitcast(I32), 0)
         load_scale_rows(w2_plane, w2_scales)
         l3 = load_list(offs3, "l3")
         sa_sb = keep.tile([P, PACK], F32, name="sa_sb")
@@ -133,8 +132,8 @@ def tile_list_twoownboards_twow_one_owntwopages_kernel(
         l6 = load_list(offs6, "l6")
         l7 = load_list(offs7, "l7")
 
-        w2_codes = keep.tile([P, R], I32, name="w2_codes", align_bytes=64)
-        w2_sc = keep.tile([P, R], U8, name="w2_sc", align_bytes=64)
+        w2_codes = keep.tile([P, R], I32, name="w2_codes", tag="xt_tab", align_bytes=64)
+        w2_sc = keep.tile([P, R], U8, name="w2_sc", tag="xt_plane", align_bytes=64)
         nc.vector.tensor_copy(
             w2_codes[:].rearrange("p (t m) -> p m t", t=PACK), w2_raw[:].rearrange("p (m t) -> p m t", t=PACK)
         )
@@ -146,50 +145,52 @@ def tile_list_twoownboards_twow_one_owntwopages_kernel(
         pv = []
         for t in range(PACK):
             product(w2_codes[:, P * t : P * (t + 1)].bitcast(E4M3X4), w2_sc[:, P * t : P * (t + 1)], slice(0, J), b_sb[t][:])
-            pv.append(page("pv%d" % t, ("xt_tab", "xt_plane", "w_raw", "w_plane")[t]))
+            pv.append(page("pv%d" % t, ("w2_plane", "w2_raw", "w_raw", "w_plane")[t]))
 
         def fetch(picked, t, h):
             nc.scalar.activation(picked[:, 0, t, :], pw[t][:].indirect(half(l4, h)), COPY, scale=sa_sb[:, t : t + 1])
             nc.scalar.activation(picked[:, 1, t, :], pv[t][:].indirect(half(l5, h)), COPY, scale=sb_sb[:, t : t + 1])
 
         def subtract(diff, picked, ts):
-            nc.vector.tensor_tensor(diff[:, ts, :], picked[:, 0, ts, :], picked[:, 1, ts, :], ALU.subtract)
+            nc.vector.tensor_tensor(diff, picked[:, 0, ts, :], picked[:, 1, ts, :], ALU.subtract)
 
         def magnitude(hid, diff, ts):
-            d = diff[:, ts, :].rearrange("p t o -> p o t")
+            d = diff[:].rearrange("p t o -> p o t")
             nc.vector.scalar_tensor_tensor(hid[:, :, ts], d, -1.0, d, ALU.mult, ALU.max)
 
         def quantise(picked, h):
-            diff = keep.tile([P, PACK, HALF], F32, name="diff%d" % h)
-            hid = keep.tile([P, HALF, PACK], BF16, name="hid%d" % h, align_bytes=64)
-            subtract(diff, picked, slice(0, 2))
-            magnitude(hid, diff, slice(0, 2))
-            subtract(diff, picked, slice(2, 3))
-            subtract(diff, picked, slice(3, 4))
-            magnitude(hid, diff, slice(2, 4))
-            codes = keep.tile([P, HALF], U32, name="hid_codes%d" % h, align_bytes=64)
+            tags = (("low0", "high0"), ("hid0", "hid_codes0"))[h]
+            low = keep.tile([P, 2, HALF], F32, name="low%d" % h, tag=tags[0], align_bytes=64)
+            hid = keep.tile([P, HALF, PACK], BF16, name="hid%d" % h, tag="hid%d" % h, align_bytes=64)
+            subtract(low[:], picked, slice(0, 2))
+            magnitude(hid, low, slice(0, 2))
+            high = keep.tile([P, 2, HALF], F32, name="high%d" % h, tag=tags[1], align_bytes=64)
+            subtract(high[:, 0:1, :], picked, slice(2, 3))
+            subtract(high[:, 1:2, :], picked, slice(3, 4))
+            magnitude(hid, high, slice(2, 4))
+            codes = keep.tile([P, HALF], U32, name="hid_codes%d" % h, tag="hid_codes%d" % h, align_bytes=64)
             scales = keep.tile([P, HALF], U8, name="hid_sc%d" % h, align_bytes=64)
             nc.vector.quantize_mx(out=codes[:].bitcast(E4M3X4), scales=scales[:], in_=hid[:].rearrange("p o t -> p (o t)"))
             return codes, scales
 
         def output_product(codes, scales, h):
-            acc = second.tile([P, 2, HALF], F32, name="acc2_%d" % h)
+            p_sb = keep.tile([P, 2, HALF], F32, name="p_sb%d" % h)
             for m in range(2):
+                acc = second.tile([P, HALF], F32, name="acc2_%d%d" % (h, m))
                 nc.tensor.matmul_mx(
-                    out=acc[:, m, :], lhsT=wb_codes[:, 2 * P * m : 2 * P * (m + 1)].bitcast(E2M1X4),
+                    out=acc[:], lhsT=wb_codes[:, 2 * P * m : 2 * P * (m + 1)].bitcast(E2M1X4),
                     lhsT_scale=wb_sc[:, P * m : P * (m + 1)],
                     rhs=codes[:].bitcast(E4M3X4), rhs_scale=scales[:], start=True, stop=True,
                 )
-            p_sb = keep.tile([P, 2, HALF], F32, name="p_sb%d" % h)
-            nc.vector.tensor_copy(p_sb[:], acc[:])
+                nc.vector.tensor_copy(p_sb[:, m, :], acc[:])
             return p_sb
 
         picked0 = keep.tile([P, 2, PACK, HALF], F32, name="picked0")
         for t in range(PACK):
             nc.scalar.activation(pv[t][:].indirect(l3[:]), b_sb[t][:], COPY)
             fetch(picked0, t, 0)
-        pa = [page("pa%d" % m, ("w2_raw", "w2_plane")[m]) for m in range(2)]
-        pb = [page("pb%d" % m, ("w_codes", "w_sc")[m]) for m in range(2)]
+        pa = [page("pa%d" % m, ("xt_tab", "xt_plane")[m]) for m in range(2)]
+        pb = [page("pb%d" % m, ("w_codes", "w_sc0")[m]) for m in range(2)]
         p0 = output_product(*quantise(picked0, 0), 0)
 
         picked1 = keep.tile([P, 2, PACK, HALF], F32, name="picked1", tag="b_sb3")
@@ -206,6 +207,8 @@ def tile_list_twoownboards_twow_one_owntwopages_kernel(
             nc.scalar.activation(pa[m][:].indirect(half(l6, 1)), p1[:, m, :], COPY)
             nc.vector.tensor_copy(pb[m][:].indirect(half(l7, 1)), p1[:, m, :])
         for m in range(2):
-            res = keep.tile([P, E], F32, name="res%d" % m)
-            nc.vector.tensor_tensor(res[:], pa[m][:], pb[m][:], ALU.add)
-            nc.sync.dma_start(out[P * m : P * (m + 1), :], res[:])
+            for c, queue in enumerate((nc.sync, nc.scalar)):
+                cols = slice(c * E // 2, (c + 1) * E // 2)
+                res = keep.tile([P, E // 2], F32, name="res%d%d" % (m, c))
+                nc.vector.tensor_tensor(res[:], pa[m][:, cols], pb[m][:, cols], ALU.add)
+                queue.dma_start(out[P * m : P * (m + 1), cols], res[:])

@@ -47,6 +47,7 @@ def tile_list_twoownboards_twow_one_owntwopages_kernel(
                 nc.sync.dma_start(plane[32 * q : 32 * q + 4, :].bitcast(I32), src[0, 4 * q : 4 * q + 4, :].bitcast(I32))
 
         xt_plane = keep.tile([P, T], U8, name="xt_plane", tag="xt_plane", align_bytes=64)
+        nc.gpsimd.memset(xt_plane[:].bitcast(I32), 0)
         w_plane = keep.tile([P, R], U8, name="w_plane", tag="w_plane", align_bytes=64)
         nc.vector.memset(w_plane[:].bitcast(I32), 0)
 
@@ -60,9 +61,7 @@ def tile_list_twoownboards_twow_one_owntwopages_kernel(
         l1 = load_list(offs, "l1")
         nc.scalar.dma_start(xt_tab[:].bitcast(I32), xt_words[0].rearrange("p n t -> p (n t)").bitcast(I32))
         nc.scalar.dma_start(w_raw[:].bitcast(I32), w_words[0].bitcast(I32))
-        for q in range(4):
-            rows = xt_scales[0, 4 * q : 4 * q + 4, :].bitcast(I32)
-            nc.sync.dma_start(xt_plane[32 * q : 32 * q + 32, :].bitcast(I32), rows.unsqueeze(0).to_broadcast([8, 4, T // 4]))
+        load_scale_rows(xt_plane, xt_scales)
         l2 = load_list(offs2, "l2")
 
         for q in range(4):
@@ -196,13 +195,13 @@ def tile_list_twoownboards_twow_one_owntwopages_kernel(
         picked1 = keep.tile([P, 2, PACK, HALF], F32, name="picked1", tag="b_sb3")
         for t in range(PACK):
             fetch(picked1, t, 1)
-        hid1 = quantise(picked1, 1)
-        nc.vector.tensor_copy(pb[0][:].indirect(half(l7, 0)), p0[:, 0, :])
-        p1 = output_product(*hid1, 1)
+        p1 = output_product(*quantise(picked1, 1), 1)
 
         for m in range(2):
             nc.scalar.activation(pa[m][:].indirect(half(l6, 0)), p0[:, m, :], COPY)
-        nc.scalar.activation(pb[1][:].indirect(half(l7, 0)), p0[:, 1, :], COPY)
+        nc.vector.tensor_copy(pb[1][:].indirect(l7[:, 4:8]), p0[:, 1, 64:128])
+        nc.scalar.activation(pb[0][:].indirect(half(l7, 0)), p0[:, 0, :], COPY)
+        nc.scalar.activation(pb[1][:].indirect(l7[:, 0:4]), p0[:, 1, 0:64], COPY)
         for m in range(2):
             nc.scalar.activation(pa[m][:].indirect(half(l6, 1)), p1[:, m, :], COPY)
             nc.vector.tensor_copy(pb[m][:].indirect(half(l7, 1)), p1[:, m, :])

from contextlib import ExitStack

import concourse.mybir as mybir

K, T, J, R, C, O, N, E = 512, 1024, 256, 512, 512, 256, 256, 512
FLOPS = 2 * K * R * J * 2 + 2 * R * N * O

F32 = mybir.dt.float32
BF16 = mybir.dt.bfloat16
I32 = mybir.dt.int32
U32 = mybir.dt.uint32
U16 = mybir.dt.uint16
U8 = mybir.dt.uint8
E4M3X4 = mybir.dt.float8_e4m3fn_x4
E5M2X4 = mybir.dt.float8_e5m2_x4
E2M1X4 = mybir.dt.float4_e2m1fn_x4
COPY = mybir.ActivationFunctionType.Copy
ALU = mybir.AluOpType

P = 128
PACK = 4
HALF = 128
HALF_COLS = HALF // 16


def tile_list_twoownboards_twow_one_owntwopages_kernel(
    tc, xt_words, xt_scales, w_words, w_scales, w2_words, w2_scales, sa, sb, wb_words, wb_scales,
    offs, offs2, offs3, offs4, offs5, offs6, offs7, out,
):
    nc = tc.nc
    with ExitStack() as ctx:
        lists = ctx.enter_context(tc.tile_pool(name="lists", bufs=1))
        keep = ctx.enter_context(tc.tile_pool(name="keep", bufs=1))
        first = ctx.enter_context(tc.psum_pool(name="first", bufs=4))
        second = ctx.enter_context(tc.psum_pool(name="second", bufs=1))

        def load_list(src, name):
            t = lists.tile([P, 16], U16, name=name)
            nc.sync.dma_start(t[:], src)
            return t

        def half(lst, h):
            return lst[:, h * HALF_COLS : (h + 1) * HALF_COLS]

        def load_scale_rows(plane, src):
            for q in range(4):
                nc.sync.dma_start(plane[32 * q : 32 * q + 4, :].bitcast(I32), src[0, 4 * q : 4 * q + 4, :].bitcast(I32))

        xt_plane = keep.tile([P, T], U8, name="xt_plane", tag="xt_plane", align_bytes=64)
        nc.gpsimd.memset(xt_plane[:].bitcast(I32), 0)
        w_plane = keep.tile([P, R], U8, name="w_plane", tag="w_plane", align_bytes=64)
        nc.vector.memset(w_plane[:].bitcast(I32), 0)

        w2_plane = keep.tile([P, R], U8, name="w2_plane", tag="w2_plane", align_bytes=64)
        nc.vector.memset(w2_plane[:].bitcast(I32), 0)
        xt_tab = keep.tile([P, T], U32, name="xt_tab", tag="xt_tab", align_bytes=64)
        w_raw = keep.tile([P, 2 * R], U8, name="w_raw", tag="w_raw", align_bytes=64)

        w_stage = keep.tile([4, 4, R // 4], I32, name="w_stage", align_bytes=64)
        nc.sync.dma_start(w_stage[:], w_scales[0].bitcast(I32).rearrange("(q r) c -> r q c", q=4))
        l1 = load_list(offs, "l1")
        nc.scalar.dma_start(xt_tab[:].bitcast(I32), xt_words[0].rearrange("p n t -> p (n t)").bitcast(I32))
        nc.scalar.dma_start(w_raw[:].bitcast(I32), w_words[0].bitcast(I32))
        load_scale_rows(xt_plane, xt_scales)
        l2 = load_list(offs2, "l2")

        for q in range(4):
            nc.vector.tensor_copy(w_plane[32 * q : 32 * q + 4, :].bitcast(I32), w_stage[:, q, :])

        w_codes0 = keep.tile([P, 2 * P], U8, name="w_codes0", align_bytes=64)
        w_sc0 = keep.tile([P, P], U8, name="w_sc0", tag="w_sc0", align_bytes=64)
        w_codes = keep.tile([P, 2 * (R - P)], U8, name="w_codes", tag="w_codes", align_bytes=64)
        w_raw_tm = w_raw[:].bitcast(U16).rearrange("p (m t) -> p t m", t=PACK)
        w_codes_tm = w_codes[:].bitcast(U16).rearrange("p (t m) -> p t m", t=PACK - 1)
        w_plane_tm = w_plane[:].rearrange("p (m t) -> p t m", t=PACK)
        nc.scalar.copy(w_codes0[:].bitcast(U16), w_raw_tm[:, 0, :])
        nc.vector.tensor_copy(w_sc0[:], w_plane_tm[:, 0, :])

        xg = keep.tile([P, J], U32, name="xg", align_bytes=64)
        xg_sc = keep.tile([P, J], U8, name="xg_sc", align_bytes=64)

        def page(name, tag):
            t = keep.tile([P, C], F32, name=name, tag=tag, align_bytes=64)
            nc.vector.memset(t[:], 0.0)
            return t

        def product(codes, scales, cols, dst):
            width = cols.stop - cols.start
            acc = first.tile([P, width], F32, name="acc")
            nc.tensor.matmul_mx(
                out=acc[:], lhsT=codes, lhsT_scale=scales,
                rhs=xg[:, cols].bitcast(E5M2X4), rhs_scale=xg_sc[:, cols], start=True, stop=True,
            )
            nc.vector.tensor_copy(dst, acc[:])

        def w_slice(t):
            return w_codes[:, 2 * P * (t - 1) : 2 * P * t].bitcast(E2M1X4), w_sc[:, P * (t - 1) : P * t]

        a_sb = [keep.tile([P, J], F32, name="a_sb%d" % t) for t in range(PACK)]
        pw = [page("pw0", "pw0")]
        for h in range(2):
            cols = slice(h * HALF, (h + 1) * HALF)
            nc.vector.tensor_copy(xg_sc[:, cols], xt_plane[:].indirect(half(l1, h)))
            nc.vector.tensor_copy(xg[:, cols], xt_tab[:].indirect(half(l1, h)))
            product(w_codes0[:].bitcast(E2M1X4), w_sc0[:], cols, a_sb[0][:, cols])
            nc.scalar.activation(pw[0][:].indirect(half(l2, h)), a_sb[0][:, cols], COPY)
            if h == 0:
                nc.scalar.copy(w_codes_tm, w_raw_tm[:, 1:, :])
        w_sc = keep.tile([P, R - P], U8, name="w_sc", tag="xt_plane", align_bytes=64)
        nc.vector.tensor_copy(w_sc[:].rearrange("p (t m) -> p t m", t=PACK - 1), w_plane_tm[:, 1:, :])
        for t in range(1, PACK):
            product(*w_slice(t), slice(0, J), a_sb[t][:])
            pw.append(page("pw%d" % t, "pw%d" % t))
            nc.scalar.activation(pw[t][:].indirect(l2[:]), a_sb[t][:], COPY)

        w2_raw = keep.tile([P, R], I32, name="w2_raw", tag="w2_raw", align_bytes=64)
        nc.sync.dma_start(w2_raw[:], w2_words[0].rearrange("p n t -> p (n t)").bitcast(I32))
        load_scale_rows(w2_plane, w2_scales)
        l3 = load_list(offs3, "l3")
        sa_sb = keep.tile([P, PACK], F32, name="sa_sb")
        nc.sync.dma_start(sa_sb[:], sa.rearrange("(p t) o -> p (t o)", t=PACK))
        sb_sb = keep.tile([P, PACK], F32, name="sb_sb")
        nc.sync.dma_start(sb_sb[:], sb.rearrange("(p t) o -> p (t o)", t=PACK))
        l4 = load_list(offs4, "l4")
        l5 = load_list(offs5, "l5")
        wb_codes = keep.tile([P, 2 * N], U8, name="wb_codes", align_bytes=64)
        nc.sync.dma_start(wb_codes[:].bitcast(I32), wb_words[0].bitcast(I32))
        wb_sc = keep.tile([P, N], U8, name="wb_sc", align_bytes=64)
        nc.vector.memset(wb_sc[:].bitcast(I32), 0)
        load_scale_rows(wb_sc, wb_scales)
        l6 = load_list(offs6, "l6")
        l7 = load_list(offs7, "l7")

        w2_codes = keep.tile([P, R], I32, name="w2_codes", tag="xt_tab", align_bytes=64)
        w2_sc = keep.tile([P, R], U8, name="w2_sc", tag="xt_plane", align_bytes=64)
        nc.vector.tensor_copy(
            w2_codes[:].rearrange("p (t m) -> p m t", t=PACK), w2_raw[:].rearrange("p (m t) -> p m t", t=PACK)
        )
        nc.vector.tensor_copy(
            w2_sc[:].rearrange("p (t m) -> p m t", t=PACK), w2_plane[:].rearrange("p (m t) -> p m t", t=PACK)
        )

        b_sb = [keep.tile([P, J], F32, name="b_sb%d" % t, tag="b_sb%d" % t) for t in range(PACK)]
        pv = []
        for t in range(PACK):
            product(w2_codes[:, P * t : P * (t + 1)].bitcast(E4M3X4), w2_sc[:, P * t : P * (t + 1)], slice(0, J), b_sb[t][:])
            pv.append(page("pv%d" % t, ("w2_plane", "w2_raw", "w_raw", "w_plane")[t]))

        def fetch(picked, t, h):
            nc.scalar.activation(picked[:, 0, t, :], pw[t][:].indirect(half(l4, h)), COPY, scale=sa_sb[:, t : t + 1])
            nc.scalar.activation(picked[:, 1, t, :], pv[t][:].indirect(half(l5, h)), COPY, scale=sb_sb[:, t : t + 1])

        def subtract(diff, picked, ts):
            nc.vector.tensor_tensor(diff, picked[:, 0, ts, :], picked[:, 1, ts, :], ALU.subtract)

        def magnitude(hid, diff, ts):
            d = diff[:].rearrange("p t o -> p o t")
            nc.vector.scalar_tensor_tensor(hid[:, :, ts], d, -1.0, d, ALU.mult, ALU.max)

        def quantise(picked, h):
            tags = (("low0", "high0"), ("hid0", "hid_codes0"))[h]
            low = keep.tile([P, 2, HALF], F32, name="low%d" % h, tag=tags[0], align_bytes=64)
            hid = keep.tile([P, HALF, PACK], BF16, name="hid%d" % h, tag="hid%d" % h, align_bytes=64)
            subtract(low[:], picked, slice(0, 2))
            magnitude(hid, low, slice(0, 2))
            high = keep.tile([P, 2, HALF], F32, name="high%d" % h, tag=tags[1], align_bytes=64)
            subtract(high[:, 0:1, :], picked, slice(2, 3))
            subtract(high[:, 1:2, :], picked, slice(3, 4))
            magnitude(hid, high, slice(2, 4))
            codes = keep.tile([P, HALF], U32, name="hid_codes%d" % h, tag="hid_codes%d" % h, align_bytes=64)
            scales = keep.tile([P, HALF], U8, name="hid_sc%d" % h, align_bytes=64)
            nc.vector.quantize_mx(out=codes[:].bitcast(E4M3X4), scales=scales[:], in_=hid[:].rearrange("p o t -> p (o t)"))
            return codes, scales

        def output_product(codes, scales, h):
            p_sb = keep.tile([P, 2, HALF], F32, name="p_sb%d" % h)
            for m in range(2):
                acc = second.tile([P, HALF], F32, name="acc2_%d%d" % (h, m))
                nc.tensor.matmul_mx(
                    out=acc[:], lhsT=wb_codes[:, 2 * P * m : 2 * P * (m + 1)].bitcast(E2M1X4),
                    lhsT_scale=wb_sc[:, P * m : P * (m + 1)],
                    rhs=codes[:].bitcast(E4M3X4), rhs_scale=scales[:], start=True, stop=True,
                )
                nc.vector.tensor_copy(p_sb[:, m, :], acc[:])
            return p_sb

        picked0 = keep.tile([P, 2, PACK, HALF], F32, name="picked0")
        for t in range(PACK):
            nc.scalar.activation(pv[t][:].indirect(l3[:]), b_sb[t][:], COPY)
            fetch(picked0, t, 0)
        pa = [page("pa%d" % m, ("xt_tab", "xt_plane")[m]) for m in range(2)]
        pb = [page("pb%d" % m, ("w_codes", "w_sc0")[m]) for m in range(2)]
        p0 = output_product(*quantise(picked0, 0), 0)

        picked1 = keep.tile([P, 2, PACK, HALF], F32, name="picked1", tag="b_sb3")
        for t in range(PACK):
            fetch(picked1, t, 1)
        p1 = output_product(*quantise(picked1, 1), 1)

        for m in range(2):
            nc.scalar.activation(pa[m][:].indirect(half(l6, 0)), p0[:, m, :], COPY)
        nc.vector.tensor_copy(pb[1][:].indirect(l7[:, 4:8]), p0[:, 1, 64:128])
        nc.scalar.activation(pb[0][:].indirect(half(l7, 0)), p0[:, 0, :], COPY)
        nc.scalar.activation(pb[1][:].indirect(l7[:, 0:4]), p0[:, 1, 0:64], COPY)
        for m in range(2):
            nc.scalar.activation(pa[m][:].indirect(half(l6, 1)), p1[:, m, :], COPY)
            nc.vector.tensor_copy(pb[m][:].indirect(half(l7, 1)), p1[:, m, :])
        for m in range(2):
            for c, queue in enumerate((nc.sync, nc.scalar)):
                cols = slice(c * E // 2, (c + 1) * E // 2)
                res = keep.tile([P, E // 2], F32, name="res%d%d" % (m, c))
                nc.vector.tensor_tensor(res[:], pa[m][:, cols], pb[m][:, cols], ALU.add)
                queue.dma_start(out[P * m : P * (m + 1), cols], res[:])
